import numpy as np
import ml_dtypes


def mxq(x, axis, fmt="e4m3"):
    dtype, down = {"e4m3": (ml_dtypes.float8_e4m3fn, 7), "e5m2": (ml_dtypes.float8_e5m2, 14)}[fmt]
    v = np.moveaxis(np.asarray(x, np.float32).astype(ml_dtypes.bfloat16).astype(np.float64), axis, -1)
    blocks = v.reshape(v.shape[:-1] + (-1, 32))
    amax = np.abs(blocks).max(-1, keepdims=True)
    byte = np.maximum(np.where(amax > 0, np.frexp(amax)[1] - 1 + 127, 0) - down, 1)
    scale = np.exp2(byte - 127.0)
    codes = (blocks / scale).astype(np.float32).astype(dtype).astype(np.float64)
    return np.moveaxis((codes * scale).reshape(v.shape), -1, axis)


WIDE = False


def mx_kscale(k):
    if not WIDE:
        return np.ones(k)
    levels = np.array([10, -10, 5, -5, 0])
    if k % 512:
        return np.exp2(np.random.permutation(np.resize(levels, k // 32))).repeat(32)
    a = np.empty((k // 512, 16))
    for p in range(k // 512):
        a[p, :8] = np.random.permutation(np.resize(levels, 8))
        for g in range(8):
            far = levels[np.abs(levels - a[p, g]) >= 10]
            a[p, g + 8] = far[np.random.randint(len(far))]
    return np.exp2(a.ravel()).repeat(32)


def f64(x):
    return np.asarray(x).astype(np.float64)


def striped(idx):
    return np.tile(np.asarray(idx).reshape(-1, 16).T, (8, 1)).astype(np.uint16)


def unstriped(offs):
    return offs[:16].T.reshape(-1).astype(np.int64)


E2M1 = np.array([0.0, 0.5, 1.0, 1.5, 2.0, 3.0, 4.0, 6.0, -0.0, -0.5, -1.0, -1.5, -2.0, -3.0, -4.0, -6.0])


def pack_weight(w, fmt):
    k, n = w.shape
    w = f64(np.asarray(w, np.float32).astype(ml_dtypes.bfloat16)).reshape(k // 32, 32, n)
    amax = np.abs(w).max(1)
    if fmt == "e4m3":
        byte = np.frexp(amax)[1] - 1 + 127 - 7
    else:
        mant, ex = np.frexp(amax / 6.0)
        byte = np.where(mant > 0.5, ex, ex - 1) + 127
    byte = np.clip(np.where(amax > 0, byte, 1), 1, 254)
    scaled = (w * np.exp2(127.0 - byte)[:, None, :]).reshape(k, n).astype(np.float32)
    by_word = np.ascontiguousarray(scaled.reshape(k // 512, 128, 4, n).transpose(0, 1, 3, 2))
    if fmt == "e4m3":
        words = by_word.astype(ml_dtypes.float8_e4m3fn).view(np.uint8)
    else:
        c = by_word.astype(ml_dtypes.float4_e2m1fn).view(np.uint8) & 0xF
        words = (c[..., 0::2] | (c[..., 1::2] << 4)).reshape(k // 512, 128, 2 * n)
    return np.ascontiguousarray(words), np.ascontiguousarray(byte.astype(np.uint8).reshape(k // 512, 16, n))


def unpack_weight(words, scales, fmt):
    g, _, n = scales.shape
    words = np.ascontiguousarray(words).reshape(g, 128, n, -1)
    if fmt == "e4m3":
        vals = words.view(ml_dtypes.float8_e4m3fn).astype(np.float64)
    else:
        nib = np.empty((g, 128, n, 4), np.uint8)
        nib[..., 0::2] = words & 0xF
        nib[..., 1::2] = words >> 4
        vals = E2M1[nib]
    vals = vals * np.repeat(np.exp2(scales.astype(np.float64) - 127.0), 8, axis=1)[..., None]
    return vals.transpose(0, 1, 3, 2).reshape(g * 512, n)


K, T, J, N, R = 1024, 2048, 512, 512, 512


def setup_inputs():
    n = np.random.standard_normal
    idx = np.random.permutation(T)[:J]
    fk = mx_kscale(K)
    fr = mx_kscale(R)
    xtp = pack_weight(n((K, T)) / fk[:, None], "e4m3")
    wap = pack_weight(n((K, R)) * 1 / np.sqrt(K) * fk[:, None] * fr, "e2m1")
    wbp = pack_weight(n((K, R)) * 1 / np.sqrt(K) * fk[:, None] * fr, "e4m3")
    wdp = pack_weight(n((R, N)) * 1 / np.sqrt(R) / fr[:, None], "e2m1")
    return {
        "xt_words": xtp[0],
        "xt_scales": xtp[1],
        "wa_words": wap[0],
        "wa_scales": wap[1],
        "wb_words": wbp[0],
        "wb_scales": wbp[1],
        "wd_words": wdp[0],
        "wd_scales": wdp[1],
        "ga": (np.random.uniform(0.4, 1.2, (1, J))).astype(np.float32),
        "offs": striped(idx),
    }


def reference(xt_words, xt_scales, wa_words, wa_scales, wb_words, wb_scales, wd_words, wd_scales, ga, offs):
    idx = unstriped(offs)
    xtu = unpack_weight(xt_words, xt_scales, "e4m3")
    wau = unpack_weight(wa_words, wa_scales, "e2m1")
    wbu = unpack_weight(wb_words, wb_scales, "e4m3")
    wdu = unpack_weight(wd_words, wd_scales, "e2m1")
    xtidxg = xtu[:, idx]
    a = wau.T @ xtidxg
    b = wbu.T @ xtidxg
    hid = np.maximum(a - b, 0.0)
    hidq = mxq(hid, 0, "e4m3")
    p = wdu.T @ hidq
    y = p * f64(ga)
    return y

@@ -1,0 +1,179 @@
+from contextlib import ExitStack
+
+import concourse.mybir as mybir
+from concourse.masks import make_identity
+
+K, T, J, N, R = 1024, 2048, 512, 512, 512
+FLOPS = 2 * 2 * K * R * J + 2 * R * N * J
+
+F32 = mybir.dt.float32
+BF16 = mybir.dt.bfloat16
+I32 = mybir.dt.int32
+U32 = mybir.dt.uint32
+U16 = mybir.dt.uint16
+U8 = mybir.dt.uint8
+FP8X4 = mybir.dt.float8_e4m3fn_x4
+FP4X4 = mybir.dt.float4_e2m1fn_x4
+ALU = mybir.AluOpType
+ACT = mybir.ActivationFunctionType
+
+P = 128
+PASSES = K // 512
+CHUNKS = J // P
+HALF = J // 2
+WB_ROW = 4
+
+
+def tile_moe_experts_difference_hidden_kernel(
+    tc, xt_words, xt_scales, wa_words, wa_scales, wb_words, wb_scales, wd_words, wd_scales, ga, offs, out
+):
+    nc = tc.nc
+    with ExitStack() as ctx:
+        keep = ctx.enter_context(tc.tile_pool(name="keep", bufs=1))
+        psum = ctx.enter_context(tc.psum_pool(name="psum", bufs=1))
+
+        offsets = keep.tile([P, J // 16], U16, name="offsets")
+        ga_col = keep.tile([P, 4], F32, name="ga_col")
+        x_planes = keep.tile([P, PASSES, T], U8, name="x_planes", align_bytes=64)
+        w_planes = keep.tile([P, PASSES + 1, R], U8, name="w_planes", align_bytes=64)
+        ident = keep.tile([P, P], F32, name="ident", align_bytes=64)
+        x_win = [keep.tile([P, T], I32, name=f"x_win{z}", align_bytes=64) for z in range(PASSES)]
+        wa = keep.tile([P, PASSES, 2 * R], U8, name="wa", align_bytes=64)
+        wb = [keep.tile([P, R], I32, name=f"wb{z}", align_bytes=64) for z in range(PASSES)]
+        wd = keep.tile([P, 2 * N], U8, name="wd", align_bytes=64)
+
+        nc.vector.memset(x_planes[:].rearrange("p z c -> p (z c)").bitcast(I32), 0)
+        nc.vector.memset(w_planes[:].rearrange("p z c -> p (z c)").bitcast(I32), 0)
+        nc.vector.memset(ident[:], 0.0)
+
+        def load_rows(queue, planes, first, scales):
+            for r in range(4):
+                queue.dma_start(
+                    out=planes[first + r : P : 32].bitcast(I32),
+                    in_=scales[:, r:16:4, :].rearrange("z q c -> q z c").bitcast(I32),
+                )
+
+        def words(w, z):
+            return w[z].rearrange("p c t -> p (c t)").bitcast(I32)
+
+        load_rows(nc.sync, x_planes[:], 0, xt_scales)
+        load_rows(nc.scalar, w_planes[:, 0:PASSES, :], 0, wa_scales)
+        load_rows(nc.scalar, w_planes[:, 0:PASSES, :], WB_ROW, wb_scales)
+        make_identity(nc, ident[:], nomemset=True)
+        nc.sync.dma_start(offsets[:], offs)
+        nc.sync.dma_start(out=ga_col[:], in_=ga.rearrange("o (p m) -> (o p) m", m=4))
+        nc.sync.dma_start(out=wb[0][:], in_=words(wb_words, 0))
+        nc.sync.dma_start(out=wa[:].bitcast(I32), in_=wa_words.rearrange("z p b -> p z b").bitcast(I32))
+        nc.sync.dma_start(out=x_win[0][:], in_=words(xt_words, 0))
+        nc.sync.dma_start(out=x_win[1][:], in_=words(xt_words, 1))
+        nc.sync.dma_start(out=wb[1][:], in_=words(wb_words, 1))
+        nc.sync.dma_start(out=wd[:].bitcast(I32), in_=wd_words[0].bitcast(I32))
+        load_rows(nc.sync, w_planes[:, PASSES : PASSES + 1, :], 0, wd_scales)
+
+        ga_bank = psum.tile([P, 4, P], F32, name="ga_bank", tag="a3")
+        for m in range(4):
+            nc.tensor.transpose(ga_bank[:, m, :], ga_col[:, m : m + 1].to_broadcast([P, P]), ident[:])
+        ga_rows = keep.tile([P, J], F32, name="ga_rows")
+        nc.scalar.activation(
+            out=ga_rows[:].rearrange("i (p m) -> i p m", m=4), in_=ga_bank[:].rearrange("i m p -> i p m"), func=ACT.Copy
+        )
+
+        xg_planes = [keep.tile([P, J], U8, name=f"xg_planes{z}", align_bytes=64) for z in range(PASSES)]
+        xg = [keep.tile([P, J], U32, name=f"xg{z}", align_bytes=64) for z in range(PASSES)]
+        for z in range(PASSES):
+            nc.vector.tensor_copy(xg_planes[z][:], x_planes[:, z, :].indirect(offsets[:]))
+        for z in range(PASSES):
+            for h in range(2):
+                nc.vector.tensor_copy(
+                    xg[z][:, h * HALF : (h + 1) * HALF],
+                    x_win[z][:].bitcast(U32).indirect(offsets[:, h * HALF // 16 : (h + 1) * HALF // 16]),
+                )
+
+        a_bank = [psum.tile([P, R], F32, name=f"a_bank{c}", tag=f"a{c}") for c in range(CHUNKS)]
+        b_bank = [psum.tile([P, R], F32, name=f"b_bank{c}", tag=f"b{c}") for c in range(CHUNKS)]
+        for z in range(PASSES):
+            for c in range(CHUNKS):
+                tok = slice(c * P, (c + 1) * P)
+                nc.tensor.matmul_mx(
+                    out=b_bank[c][:],
+                    lhsT=xg[z][:, tok].bitcast(FP8X4),
+                    lhsT_scale=xg_planes[z][:, tok],
+                    rhs=wb[z][:].bitcast(FP8X4),
+                    rhs_scale=w_planes[WB_ROW:P, z, :],
+                    start=(z == 0),
+                    stop=(z == PASSES - 1),
+                )
+                nc.tensor.matmul_mx(
+                    out=a_bank[c][:],
+                    lhsT=xg[z][:, tok].bitcast(FP8X4),
+                    lhsT_scale=xg_planes[z][:, tok],
+                    rhs=wa[:, z, :].bitcast(FP4X4),
+                    rhs_scale=w_planes[:, z, :],
+                    start=(z == 0),
+                    stop=(z == PASSES - 1),
+                )
+
+        b_sb, gap, hid, codes, h_planes, turned, p_bank = {}, {}, {}, {}, {}, {}, {}
+
+        def copy_b(c):
+            b_sb[c] = keep.tile([P, R], F32, name=f"b_sb{c}")
+            nc.scalar.copy(
+                out=b_sb[c][:].rearrange("j (u m e) -> j u m e", u=2, e=2),
+                in_=b_bank[c][:].rearrange("j (m u e) -> j u m e", u=2, e=2),
+            )
+
+        def subtract(c):
+            gap[c] = keep.tile([P, R], BF16, name=f"gap{c}", align_bytes=64)
+            nc.vector.tensor_tensor(
+                out=gap[c][:].rearrange("j (u m e) -> j u m e", u=2, e=2),
+                in0=a_bank[c][:].rearrange("j (m u e) -> j u m e", u=2, e=2),
+                in1=b_sb[c][:].rearrange("j (u m e) -> j u m e", u=2, e=2),
+                op=ALU.subtract,
+            )
+
+        def turn(c):
+            turned[c] = psum.tile([P, 2 * P], F32, name=f"turned{c}", tag=f"b{c}")
+            pairs = gap[c][:].bitcast(F32)
+            for u in range(2):
+                nc.tensor.transpose(turned[c][:, u * P : (u + 1) * P], pairs[:, u * P : (u + 1) * P], ident[:])
+
+        def relu(c):
+            hid[c] = keep.tile([P, 4 * P], BF16, name=f"hid{c}", align_bytes=64)
+            nc.scalar.activation(
+                out=hid[c][:].rearrange("m (j u e) -> m j u e", u=2, e=2),
+                in_=turned[c][:].bitcast(BF16).rearrange("m (u j e) -> m j u e", u=2, e=2),
+                func=ACT.Relu,
+            )
+
+        def quantise(c):
+            codes[c] = keep.tile([P, P], U32, name=f"codes{c}", align_bytes=64)
+            h_planes[c] = keep.tile([P, P], U8, name=f"h_planes{c}", align_bytes=64)
+            nc.vector.quantize_mx(out=codes[c][:].bitcast(FP8X4), scales=h_planes[c][:], in_=hid[c][:])
+
+        def project(c):
+            p_bank[c] = psum.tile([P, 4, P], F32, name=f"p_bank{c}", tag=f"a{c}")
+            for m in range(4):
+                nc.tensor.matmul_mx(
+                    out=p_bank[c][:, m, :],
+                    lhsT=wd[:, 2 * P * m : 2 * P * (m + 1)].bitcast(FP4X4),
+                    lhsT_scale=w_planes[:, PASSES, P * m : P * (m + 1)],
+                    rhs=codes[c][:].bitcast(FP8X4),
+                    rhs_scale=h_planes[c][:],
+                    start=True,
+                    stop=True,
+                )
+
+        def finish(c):
+            tok = slice(c * P, (c + 1) * P)
+            y = keep.tile([P, 4, P], F32, name=f"y{c}")
+            nc.vector.tensor_tensor(
+                out=y[:], in0=p_bank[c][:], in1=ga_rows[:, tok].unsqueeze(1).to_broadcast([P, 4, P]), op=ALU.mult
+            )
+            nc.sync.dma_start(out=out.rearrange("(m p) j -> p m j", p=P)[:, :, tok], in_=y[:])
+
+        stages = [copy_b, subtract, turn, relu, quantise, project, finish]
+        lags = [0, 0, 1, 2, 2, 2, 3]
+        for step in range(CHUNKS + 3):
+            for stage, lag in zip(stages, lags):
+                if 0 <= step - lag < CHUNKS:
+                    stage(step - lag)

@@ -1,7 +1,6 @@
 from contextlib import ExitStack
 
 import concourse.mybir as mybir
-from concourse.masks import make_identity
 
 K, T, J, N, R = 1024, 2048, 512, 512, 512
 FLOPS = 2 * 2 * K * R * J + 2 * R * N * J
@@ -30,21 +29,21 @@ def tile_moe_experts_difference_hidden_kernel(
     nc = tc.nc
     with ExitStack() as ctx:
         keep = ctx.enter_context(tc.tile_pool(name="keep", bufs=1))
+        shared = ctx.enter_context(tc.tile_pool(name="shared", bufs=1))
         psum = ctx.enter_context(tc.psum_pool(name="psum", bufs=1))
 
         offsets = keep.tile([P, J // 16], U16, name="offsets")
         ga_col = keep.tile([P, 4], F32, name="ga_col")
-        x_planes = keep.tile([P, PASSES, T], U8, name="x_planes", align_bytes=64)
-        w_planes = keep.tile([P, PASSES + 1, R], U8, name="w_planes", align_bytes=64)
+        x_planes = shared.tile([P, PASSES, T], U8, name="x_planes", align_bytes=64, offset=0)
+        w_planes = keep.tile([P, PASSES, R], U8, name="w_planes", align_bytes=64)
         ident = keep.tile([P, P], F32, name="ident", align_bytes=64)
-        x_win = [keep.tile([P, T], I32, name=f"x_win{z}", align_bytes=64) for z in range(PASSES)]
-        wa = keep.tile([P, PASSES, 2 * R], U8, name="wa", align_bytes=64)
-        wb = [keep.tile([P, R], I32, name=f"wb{z}", align_bytes=64) for z in range(PASSES)]
-        wd = keep.tile([P, 2 * N], U8, name="wd", align_bytes=64)
+        zeros = shared.tile([P, P], F32, name="zeros", align_bytes=64, offset=8192)
+        wa = [keep.tile([P, 2 * R], U8, name="wa0", align_bytes=64)]
+        wb = [keep.tile([P, R], I32, name="wb0", align_bytes=64)]
 
         nc.vector.memset(x_planes[:].rearrange("p z c -> p (z c)").bitcast(I32), 0)
         nc.vector.memset(w_planes[:].rearrange("p z c -> p (z c)").bitcast(I32), 0)
-        nc.vector.memset(ident[:], 0.0)
+        nc.vector.memset(zeros[:], 0.0)
 
         def load_rows(queue, planes, first, scales):
             for r in range(4):
@@ -57,18 +56,24 @@ def tile_moe_experts_difference_hidden_kernel(
             return w[z].rearrange("p c t -> p (c t)").bitcast(I32)
 
         load_rows(nc.sync, x_planes[:], 0, xt_scales)
-        load_rows(nc.scalar, w_planes[:, 0:PASSES, :], 0, wa_scales)
-        load_rows(nc.scalar, w_planes[:, 0:PASSES, :], WB_ROW, wb_scales)
-        make_identity(nc, ident[:], nomemset=True)
+        load_rows(nc.sync, w_planes[:], 0, wa_scales)
+        nc.gpsimd.affine_select(
+            out=ident[:],
+            in_=zeros[:],
+            compare_op=ALU.not_equal,
+            fill=1.0,
+            base=0,
+            pattern=[[-1, P]],
+            channel_multiplier=1,
+        )
         nc.sync.dma_start(offsets[:], offs)
         nc.sync.dma_start(out=ga_col[:], in_=ga.rearrange("o (p m) -> (o p) m", m=4))
         nc.sync.dma_start(out=wb[0][:], in_=words(wb_words, 0))
-        nc.sync.dma_start(out=wa[:].bitcast(I32), in_=wa_words.rearrange("z p b -> p z b").bitcast(I32))
-        nc.sync.dma_start(out=x_win[0][:], in_=words(xt_words, 0))
-        nc.sync.dma_start(out=x_win[1][:], in_=words(xt_words, 1))
-        nc.sync.dma_start(out=wb[1][:], in_=words(wb_words, 1))
-        nc.sync.dma_start(out=wd[:].bitcast(I32), in_=wd_words[0].bitcast(I32))
-        load_rows(nc.sync, w_planes[:, PASSES : PASSES + 1, :], 0, wd_scales)
+        nc.sync.dma_start(out=wa[0][:].bitcast(I32), in_=wa_words[0].bitcast(I32))
+        x_win = shared.tile([P, PASSES, T], I32, name="x_win", align_bytes=64, offset=8192)
+        nc.sync.dma_start(out=x_win[:, 0, :], in_=words(xt_words, 0))
+        load_rows(nc.sync, w_planes[:], WB_ROW, wb_scales)
+        nc.sync.dma_start(out=x_win[:, 1, :], in_=words(xt_words, 1))
 
         ga_bank = psum.tile([P, 4, P], F32, name="ga_bank", tag="a3")
         for m in range(4):
@@ -82,15 +87,34 @@ def tile_moe_experts_difference_hidden_kernel(
         xg = [keep.tile([P, J], U32, name=f"xg{z}", align_bytes=64) for z in range(PASSES)]
         for z in range(PASSES):
             nc.vector.tensor_copy(xg_planes[z][:], x_planes[:, z, :].indirect(offsets[:]))
+        wb.append(shared.tile([P, R], I32, name="wb1", align_bytes=64, offset=0))
+        wa.append(shared.tile([P, 2 * R], U8, name="wa1", align_bytes=64, offset=2048))
+        d_planes = shared.tile([P, 1, N], U8, name="d_planes", align_bytes=64, offset=3072)
+        wd = shared.tile([P, 2 * N], U8, name="wd", align_bytes=64, offset=3584)
+        nc.sync.dma_start(out=wb[1][:], in_=words(wb_words, 1))
+        nc.sync.dma_start(out=wa[1][:].bitcast(I32), in_=wa_words[1].bitcast(I32))
+        nc.sync.dma_start(out=wd[:].bitcast(I32), in_=wd_words[0].bitcast(I32))
+        nc.vector.memset(d_planes[:, 0, :].bitcast(I32), 0)
+        load_rows(nc.sync, d_planes[:], 0, wd_scales)
         for z in range(PASSES):
             for h in range(2):
                 nc.vector.tensor_copy(
                     xg[z][:, h * HALF : (h + 1) * HALF],
-                    x_win[z][:].bitcast(U32).indirect(offsets[:, h * HALF // 16 : (h + 1) * HALF // 16]),
+                    x_win[:, z, :].bitcast(U32).indirect(offsets[:, h * HALF // 16 : (h + 1) * HALF // 16]),
                 )
 
         a_bank = [psum.tile([P, R], F32, name=f"a_bank{c}", tag=f"a{c}") for c in range(CHUNKS)]
         b_bank = [psum.tile([P, R], F32, name=f"b_bank{c}", tag=f"b{c}") for c in range(CHUNKS)]
+        for warm in range(4):
+            nc.tensor.matmul_mx(
+                out=b_bank[0][:],
+                lhsT=wb[0][:, 0:P].bitcast(FP8X4),
+                lhsT_scale=xg_planes[0][:, 0:P],
+                rhs=wa[0][:].bitcast(FP4X4),
+                rhs_scale=xg_planes[0][:],
+                start=True,
+                stop=True,
+            )
         for z in range(PASSES):
             for c in range(CHUNKS):
                 tok = slice(c * P, (c + 1) * P)
@@ -107,7 +131,7 @@ def tile_moe_experts_difference_hidden_kernel(
                     out=a_bank[c][:],
                     lhsT=xg[z][:, tok].bitcast(FP8X4),
                     lhsT_scale=xg_planes[z][:, tok],
-                    rhs=wa[:, z, :].bitcast(FP4X4),
+                    rhs=wa[z][:].bitcast(FP4X4),
                     rhs_scale=w_planes[:, z, :],
                     start=(z == 0),
                     stop=(z == PASSES - 1),
@@ -156,7 +180,7 @@ def tile_moe_experts_difference_hidden_kernel(
                 nc.tensor.matmul_mx(
                     out=p_bank[c][:, m, :],
                     lhsT=wd[:, 2 * P * m : 2 * P * (m + 1)].bitcast(FP4X4),
-                    lhsT_scale=w_planes[:, PASSES, P * m : P * (m + 1)],
+                    lhsT_scale=d_planes[:, 0, P * m : P * (m + 1)],
                     rhs=codes[c][:].bitcast(FP8X4),
                     rhs_scale=h_planes[c][:],
                     start=True,
@@ -172,8 +196,8 @@ def tile_moe_experts_difference_hidden_kernel(
             nc.sync.dma_start(out=out.rearrange("(m p) j -> p m j", p=P)[:, :, tok], in_=y[:])
 
         stages = [copy_b, subtract, turn, relu, quantise, project, finish]
-        lags = [0, 0, 1, 2, 2, 2, 3]
-        for step in range(CHUNKS + 3):
+        lags = [0, 0, 1, 4, 4, 4, 5]
+        for step in range(CHUNKS + 5):
             for stage, lag in zip(stages, lags):
                 if 0 <= step - lag < CHUNKS:
                     stage(step - lag)

from contextlib import ExitStack

import concourse.mybir as mybir

K, T, J, N, R = 1024, 2048, 512, 512, 512
FLOPS = 2 * 2 * K * R * J + 2 * R * N * J

F32 = mybir.dt.float32
BF16 = mybir.dt.bfloat16
I32 = mybir.dt.int32
U32 = mybir.dt.uint32
U16 = mybir.dt.uint16
U8 = mybir.dt.uint8
FP8X4 = mybir.dt.float8_e4m3fn_x4
FP4X4 = mybir.dt.float4_e2m1fn_x4
ALU = mybir.AluOpType
ACT = mybir.ActivationFunctionType

P = 128
PASSES = K // 512
CHUNKS = J // P
HALF = J // 2
WB_ROW = 4


def tile_moe_experts_difference_hidden_kernel(
    tc, xt_words, xt_scales, wa_words, wa_scales, wb_words, wb_scales, wd_words, wd_scales, ga, offs, out
):
    nc = tc.nc
    with ExitStack() as ctx:
        keep = ctx.enter_context(tc.tile_pool(name="keep", bufs=1))
        shared = ctx.enter_context(tc.tile_pool(name="shared", bufs=1))
        psum = ctx.enter_context(tc.psum_pool(name="psum", bufs=1))

        offsets = keep.tile([P, J // 16], U16, name="offsets")
        ga_col = keep.tile([P, 4], F32, name="ga_col")
        x_planes = shared.tile([P, PASSES, T], U8, name="x_planes", align_bytes=64, offset=0)
        w_planes = keep.tile([P, PASSES, R], U8, name="w_planes", align_bytes=64)
        ident = keep.tile([P, P], F32, name="ident", align_bytes=64)
        zeros = shared.tile([P, P], F32, name="zeros", align_bytes=64, offset=8192)
        wa = [keep.tile([P, 2 * R], U8, name="wa0", align_bytes=64)]
        wb = [keep.tile([P, R], I32, name="wb0", align_bytes=64)]

        nc.vector.memset(x_planes[:].rearrange("p z c -> p (z c)").bitcast(I32), 0)
        nc.vector.memset(w_planes[:].rearrange("p z c -> p (z c)").bitcast(I32), 0)
        nc.vector.memset(zeros[:], 0.0)

        def load_rows(queue, planes, first, scales):
            for r in range(4):
                queue.dma_start(
                    out=planes[first + r : P : 32].bitcast(I32),
                    in_=scales[:, r:16:4, :].rearrange("z q c -> q z c").bitcast(I32),
                )

        def words(w, z):
            return w[z].rearrange("p c t -> p (c t)").bitcast(I32)

        load_rows(nc.sync, x_planes[:], 0, xt_scales)
        load_rows(nc.sync, w_planes[:], 0, wa_scales)
        nc.gpsimd.affine_select(
            out=ident[:],
            in_=zeros[:],
            compare_op=ALU.not_equal,
            fill=1.0,
            base=0,
            pattern=[[-1, P]],
            channel_multiplier=1,
        )
        nc.sync.dma_start(offsets[:], offs)
        nc.sync.dma_start(out=ga_col[:], in_=ga.rearrange("o (p m) -> (o p) m", m=4))
        nc.sync.dma_start(out=wb[0][:], in_=words(wb_words, 0))
        nc.sync.dma_start(out=wa[0][:].bitcast(I32), in_=wa_words[0].bitcast(I32))
        x_win = shared.tile([P, PASSES, T], I32, name="x_win", align_bytes=64, offset=8192)
        nc.sync.dma_start(out=x_win[:, 0, :], in_=words(xt_words, 0))
        load_rows(nc.sync, w_planes[:], WB_ROW, wb_scales)
        nc.sync.dma_start(out=x_win[:, 1, :], in_=words(xt_words, 1))

        ga_bank = psum.tile([P, 4, P], F32, name="ga_bank", tag="a3")
        for m in range(4):
            nc.tensor.transpose(ga_bank[:, m, :], ga_col[:, m : m + 1].to_broadcast([P, P]), ident[:])
        ga_rows = keep.tile([P, J], F32, name="ga_rows")
        nc.scalar.activation(
            out=ga_rows[:].rearrange("i (p m) -> i p m", m=4), in_=ga_bank[:].rearrange("i m p -> i p m"), func=ACT.Copy
        )

        xg_planes = [keep.tile([P, J], U8, name=f"xg_planes{z}", align_bytes=64) for z in range(PASSES)]
        xg = [keep.tile([P, J], U32, name=f"xg{z}", align_bytes=64) for z in range(PASSES)]
        for z in range(PASSES):
            nc.vector.tensor_copy(xg_planes[z][:], x_planes[:, z, :].indirect(offsets[:]))
        wb.append(shared.tile([P, R], I32, name="wb1", align_bytes=64, offset=0))
        wa.append(shared.tile([P, 2 * R], U8, name="wa1", align_bytes=64, offset=2048))
        d_planes = shared.tile([P, 1, N], U8, name="d_planes", align_bytes=64, offset=3072)
        wd = shared.tile([P, 2 * N], U8, name="wd", align_bytes=64, offset=3584)
        nc.sync.dma_start(out=wb[1][:], in_=words(wb_words, 1))
        nc.sync.dma_start(out=wa[1][:].bitcast(I32), in_=wa_words[1].bitcast(I32))
        nc.sync.dma_start(out=wd[:].bitcast(I32), in_=wd_words[0].bitcast(I32))
        nc.vector.memset(d_planes[:, 0, :].bitcast(I32), 0)
        load_rows(nc.sync, d_planes[:], 0, wd_scales)
        for z in range(PASSES):
            for h in range(2):
                nc.vector.tensor_copy(
                    xg[z][:, h * HALF : (h + 1) * HALF],
                    x_win[:, z, :].bitcast(U32).indirect(offsets[:, h * HALF // 16 : (h + 1) * HALF // 16]),
                )

        a_bank = [psum.tile([P, R], F32, name=f"a_bank{c}", tag=f"a{c}") for c in range(CHUNKS)]
        b_bank = [psum.tile([P, R], F32, name=f"b_bank{c}", tag=f"b{c}") for c in range(CHUNKS)]
        for warm in range(4):
            nc.tensor.matmul_mx(
                out=b_bank[0][:],
                lhsT=wb[0][:, 0:P].bitcast(FP8X4),
                lhsT_scale=xg_planes[0][:, 0:P],
                rhs=wa[0][:].bitcast(FP4X4),
                rhs_scale=xg_planes[0][:],
                start=True,
                stop=True,
            )
        for z in range(PASSES):
            for c in range(CHUNKS):
                tok = slice(c * P, (c + 1) * P)
                nc.tensor.matmul_mx(
                    out=b_bank[c][:],
                    lhsT=xg[z][:, tok].bitcast(FP8X4),
                    lhsT_scale=xg_planes[z][:, tok],
                    rhs=wb[z][:].bitcast(FP8X4),
                    rhs_scale=w_planes[WB_ROW:P, z, :],
                    start=(z == 0),
                    stop=(z == PASSES - 1),
                )
                nc.tensor.matmul_mx(
                    out=a_bank[c][:],
                    lhsT=xg[z][:, tok].bitcast(FP8X4),
                    lhsT_scale=xg_planes[z][:, tok],
                    rhs=wa[z][:].bitcast(FP4X4),
                    rhs_scale=w_planes[:, z, :],
                    start=(z == 0),
                    stop=(z == PASSES - 1),
                )

        b_sb, gap, hid, codes, h_planes, turned, p_bank = {}, {}, {}, {}, {}, {}, {}

        def copy_b(c):
            b_sb[c] = keep.tile([P, R], F32, name=f"b_sb{c}")
            nc.scalar.copy(
                out=b_sb[c][:].rearrange("j (u m e) -> j u m e", u=2, e=2),
                in_=b_bank[c][:].rearrange("j (m u e) -> j u m e", u=2, e=2),
            )

        def subtract(c):
            gap[c] = keep.tile([P, R], BF16, name=f"gap{c}", align_bytes=64)
            nc.vector.tensor_tensor(
                out=gap[c][:].rearrange("j (u m e) -> j u m e", u=2, e=2),
                in0=a_bank[c][:].rearrange("j (m u e) -> j u m e", u=2, e=2),
                in1=b_sb[c][:].rearrange("j (u m e) -> j u m e", u=2, e=2),
                op=ALU.subtract,
            )

        def turn(c):
            turned[c] = psum.tile([P, 2 * P], F32, name=f"turned{c}", tag=f"b{c}")
            pairs = gap[c][:].bitcast(F32)
            for u in range(2):
                nc.tensor.transpose(turned[c][:, u * P : (u + 1) * P], pairs[:, u * P : (u + 1) * P], ident[:])

        def relu(c):
            hid[c] = keep.tile([P, 4 * P], BF16, name=f"hid{c}", align_bytes=64)
            nc.scalar.activation(
                out=hid[c][:].rearrange("m (j u e) -> m j u e", u=2, e=2),
                in_=turned[c][:].bitcast(BF16).rearrange("m (u j e) -> m j u e", u=2, e=2),
                func=ACT.Relu,
            )

        def quantise(c):
            codes[c] = keep.tile([P, P], U32, name=f"codes{c}", align_bytes=64)
            h_planes[c] = keep.tile([P, P], U8, name=f"h_planes{c}", align_bytes=64)
            nc.vector.quantize_mx(out=codes[c][:].bitcast(FP8X4), scales=h_planes[c][:], in_=hid[c][:])

        def project(c):
            p_bank[c] = psum.tile([P, 4, P], F32, name=f"p_bank{c}", tag=f"a{c}")
            for m in range(4):
                nc.tensor.matmul_mx(
                    out=p_bank[c][:, m, :],
                    lhsT=wd[:, 2 * P * m : 2 * P * (m + 1)].bitcast(FP4X4),
                    lhsT_scale=d_planes[:, 0, P * m : P * (m + 1)],
                    rhs=codes[c][:].bitcast(FP8X4),
                    rhs_scale=h_planes[c][:],
                    start=True,
                    stop=True,
                )

        def finish(c):
            tok = slice(c * P, (c + 1) * P)
            y = keep.tile([P, 4, P], F32, name=f"y{c}")
            nc.vector.tensor_tensor(
                out=y[:], in0=p_bank[c][:], in1=ga_rows[:, tok].unsqueeze(1).to_broadcast([P, 4, P]), op=ALU.mult
            )
            nc.sync.dma_start(out=out.rearrange("(m p) j -> p m j", p=P)[:, :, tok], in_=y[:])

        stages = [copy_b, subtract, turn, relu, quantise, project, finish]
        lags = [0, 0, 1, 4, 4, 4, 5]
        for step in range(CHUNKS + 5):
            for stage, lag in zip(stages, lags):
                if 0 <= step - lag < CHUNKS:
                    stage(step - lag)
